import numpy as np
CORES = [4,132,140,148,156,164,172,180,188,196,204,212,220,228,236,244,252]
N = 17
T = 512
ROUTE = [[[1],[2],[10],[6],[14],[3],[15],[16],[0],[0],[11],[2],[0],[5],[0],[15],[4],[2],[5],[3],[10],[1],[12],[6],[14],[1],[5],[7],[7],[10],[7],[4],[8],[15],[10],[5],[12],[12],[1],[4],[16],[12],[1],[5],[7],[9],[0],[5],[3],[12],[8],[1],[16],[14],[2],[0],[6],[14],[8],[12],[6],[12],[4],[11],[11],[4],[14],[0],[4],[9],[5],[0],[10],[5],[8],[2],[4],[2],[11],[7],[15],[16],[5],[3],[6],[5],[13],[2],[1],[10],[3],[9],[5],[16],[2],[13],[13],[2],[0],[15],[14],[1],[3],[16],[12],[11],[4],[10],[16],[0],[13],[9],[2],[9],[14],[9],[5],[12],[11],[8],[5],[5],[15],[1],[4],[5],[9],[5],[5],[12],[10],[15],[2],[14],[15],[1],[11],[10],[9],[1],[0],[14],[13],[12],[13],[9],[8],[3],[1],[8],[0],[6],[10],[0],[9],[1],[0],[2],[12],[0],[11],[16],[15],[16],[15],[4],[13],[11],[7],[2],[4],[16],[6],[3],[6],[1],[1],[13],[5],[11],[15],[6],[14],[15],[10],[8],[12],[3],[2],[15],[5],[5],[15],[14],[14],[1],[3],[6],[12],[12],[14],[4],[7],[8],[10],[8],[7],[12],[16],[14],[10],[14],[13],[9],[8],[1],[13],[11],[3],[7],[12],[15],[16],[9],[13],[3],[16],[2],[10],[4],[8],[2],[16],[6],[0],[1],[10],[6],[2],[3],[16],[2],[9],[16],[11],[9],[2],[11],[1],[12],[1],[3],[1],[14],[13],[3],[5],[15],[0],[9],[13],[7],[11],[11],[10],[16],[9],[12],[2],[10],[5],[10],[3],[3],[9],[15],[15],[10],[0],[2],[16],[4],[16],[16],[15],[1],[8],[15],[6],[7],[11],[3],[13],[7],[6],[11],[9],[9],[14],[4],[15],[3],[11],[0],[9],[4],[2],[7],[1],[9],[10],[14],[11],[10],[7],[4],[3],[4],[1],[10],[13],[13],[10],[14],[10],[6],[5],[16],[7],[16],[6],[6],[2],[0],[5],[11],[11],[4],[10],[10],[6],[11],[9],[8],[10],[16],[1],[13],[12],[14],[10],[5],[7],[12],[14],[7],[10],[5],[14],[8],[14],[9],[7],[9],[12],[5],[10],[10],[0],[7],[7],[5],[7],[7],[15],[14],[2],[9],[6],[8],[7],[14],[2],[1],[8],[4],[1],[16],[3],[16],[12],[8],[5],[16],[9],[8],[8],[5],[1],[1],[7],[5],[11],[13],[11],[2],[6],[9],[9],[5],[5],[6],[4],[14],[10],[6],[13],[3],[11],[8],[15],[5],[12],[8],[8],[14],[7],[10],[1],[15],[7],[7],[3],[16],[11],[11],[4],[1],[8],[7],[2],[0],[13],[10],[8],[16],[15],[9],[15],[1],[4],[1],[2],[16],[10],[5],[10],[15],[10],[12],[15],[4],[3],[10],[15],[11],[8],[7],[12],[16],[1],[1],[16],[7],[2],[2],[15],[12],[12],[5],[7],[8],[0],[5],[16],[2],[7],[0],[2],[1],[8],[16],[15],[10],[2],[9],[14],[11],[2],[9],[7],[13],[3],[16],[2],[9],[10],[6],[12],[6],[6],[16]],[[3],[6],[1],[15],[7],[3],[0],[11],[3],[13],[5],[3],[4],[5],[11],[14],[5],[11],[0],[1],[6],[2],[4],[7],[6],[8],[7],[5],[0],[8],[11],[10],[5],[12],[2],[3],[5],[0],[13],[8],[16],[6],[8],[5],[0],[9],[4],[15],[12],[4],[10],[4],[8],[4],[9],[1],[0],[15],[9],[0],[13],[16],[3],[1],[12],[5],[7],[6],[3],[7],[10],[6],[3],[8],[5],[5],[6],[6],[1],[5],[12],[10],[15],[16],[15],[10],[14],[11],[15],[8],[7],[3],[5],[11],[11],[9],[0],[9],[1],[7],[7],[2],[2],[9],[9],[14],[13],[12],[9],[16],[12],[9],[8],[6],[11],[8],[3],[0],[11],[4],[0],[16],[14],[12],[2],[14],[9],[3],[16],[15],[13],[15],[9],[8],[15],[2],[1],[14],[10],[12],[0],[8],[16],[2],[3],[4],[6],[1],[4],[7],[7],[0],[5],[5],[10],[8],[0],[1],[7],[14],[12],[8],[11],[11],[6],[14],[13],[7],[5],[1],[13],[13],[4],[15],[14],[2],[12],[5],[2],[8],[1],[0],[16],[7],[2],[12],[4],[10],[11],[2],[7],[0],[7],[15],[6],[9],[15],[7],[11],[3],[12],[2],[6],[13],[16],[9],[14],[12],[7],[15],[7],[2],[1],[13],[5],[3],[12],[6],[14],[0],[13],[11],[8],[11],[13],[13],[10],[8],[15],[9],[13],[11],[8],[8],[7],[0],[0],[9],[4],[4],[5],[3],[16],[4],[16],[15],[11],[13],[13],[4],[9],[5],[15],[2],[15],[10],[9],[1],[1],[15],[4],[4],[10],[15],[7],[2],[12],[9],[1],[10],[11],[5],[12],[0],[4],[13],[2],[10],[9],[8],[14],[12],[7],[0],[3],[8],[3],[6],[14],[4],[13],[9],[6],[4],[0],[8],[6],[15],[1],[15],[1],[6],[4],[1],[8],[4],[12],[10],[9],[6],[4],[5],[13],[12],[10],[12],[13],[16],[11],[5],[5],[10],[1],[3],[16],[14],[5],[10],[1],[5],[1],[14],[5],[14],[4],[16],[7],[0],[11],[16],[0],[16],[6],[14],[6],[4],[4],[11],[12],[11],[4],[16],[12],[9],[16],[14],[15],[6],[5],[13],[6],[7],[14],[12],[0],[15],[0],[4],[14],[11],[12],[11],[8],[15],[11],[16],[14],[7],[6],[7],[3],[10],[1],[3],[4],[13],[3],[6],[7],[15],[10],[11],[1],[14],[10],[3],[9],[13],[16],[15],[1],[5],[12],[6],[3],[11],[9],[8],[12],[10],[0],[12],[11],[16],[4],[7],[3],[15],[3],[16],[3],[5],[2],[0],[2],[7],[5],[13],[9],[4],[9],[11],[6],[15],[6],[15],[15],[16],[8],[7],[16],[9],[1],[10],[0],[11],[2],[1],[11],[10],[10],[5],[15],[6],[10],[3],[10],[10],[10],[12],[5],[4],[15],[15],[13],[2],[16],[0],[9],[10],[2],[0],[1],[16],[12],[9],[10],[2],[16],[8],[15],[0],[12],[0],[1],[6],[0],[7],[2],[13],[14],[13],[8],[8],[10],[14],[8],[0],[12],[16],[16],[3],[6],[15],[12],[11],[11],[6],[10],[1],[2],[9]],[[7],[13],[13],[9],[0],[9],[0],[1],[9],[4],[4],[2],[10],[0],[15],[10],[3],[4],[4],[13],[15],[2],[9],[0],[3],[9],[11],[16],[16],[1],[11],[3],[9],[8],[12],[12],[7],[0],[1],[14],[10],[15],[15],[2],[8],[4],[16],[4],[0],[14],[11],[2],[3],[3],[4],[8],[9],[16],[7],[15],[6],[3],[1],[15],[6],[0],[16],[11],[6],[15],[4],[4],[8],[1],[7],[6],[1],[1],[4],[3],[2],[5],[3],[13],[9],[2],[15],[13],[5],[10],[2],[13],[11],[11],[16],[15],[13],[8],[3],[3],[9],[9],[3],[10],[14],[0],[9],[8],[3],[10],[0],[5],[15],[4],[16],[10],[4],[10],[0],[2],[14],[7],[8],[0],[14],[8],[14],[14],[11],[16],[12],[4],[4],[3],[7],[15],[6],[8],[3],[11],[0],[13],[5],[12],[0],[10],[3],[1],[3],[15],[5],[3],[14],[8],[10],[14],[5],[2],[14],[0],[11],[4],[1],[15],[4],[11],[10],[15],[13],[1],[13],[13],[3],[3],[14],[2],[0],[7],[1],[1],[7],[13],[10],[6],[9],[1],[11],[8],[10],[2],[11],[1],[6],[8],[2],[6],[4],[10],[13],[12],[3],[4],[2],[7],[9],[11],[11],[1],[10],[2],[3],[1],[3],[3],[16],[9],[6],[3],[16],[2],[3],[15],[5],[10],[12],[2],[10],[5],[7],[4],[6],[0],[0],[6],[14],[3],[15],[7],[9],[15],[16],[11],[2],[16],[2],[5],[9],[16],[2],[16],[0],[8],[13],[11],[16],[12],[4],[16],[13],[5],[1],[15],[13],[3],[10],[11],[4],[2],[15],[16],[14],[16],[9],[13],[0],[1],[3],[5],[9],[4],[14],[5],[7],[4],[0],[2],[14],[6],[2],[4],[10],[11],[13],[0],[5],[15],[13],[16],[10],[9],[4],[14],[16],[0],[8],[1],[12],[8],[10],[5],[5],[14],[13],[14],[9],[14],[0],[10],[8],[2],[3],[8],[15],[1],[14],[12],[5],[11],[11],[11],[2],[8],[2],[5],[3],[0],[2],[5],[10],[14],[13],[0],[0],[12],[0],[2],[7],[14],[11],[6],[9],[4],[2],[9],[13],[5],[0],[12],[5],[10],[16],[2],[2],[11],[10],[14],[0],[0],[8],[4],[16],[12],[7],[1],[16],[9],[15],[5],[8],[16],[13],[14],[3],[6],[16],[15],[3],[3],[14],[14],[15],[3],[8],[14],[11],[14],[1],[0],[12],[6],[6],[2],[10],[3],[1],[3],[4],[14],[5],[11],[8],[11],[4],[3],[3],[1],[14],[4],[6],[4],[15],[10],[12],[13],[13],[0],[1],[0],[16],[4],[13],[16],[15],[3],[13],[15],[12],[6],[11],[9],[16],[13],[9],[0],[16],[11],[14],[13],[0],[1],[10],[3],[12],[3],[2],[4],[15],[3],[1],[11],[13],[10],[2],[7],[11],[6],[5],[1],[11],[11],[4],[15],[0],[7],[7],[15],[7],[12],[6],[2],[10],[13],[6],[1],[10],[2],[2],[5],[12],[16],[14],[6],[4],[2],[6],[6],[4],[1],[0],[7],[2],[0],[10],[10],[9],[12],[4],[7],[8],[14],[5],[4]],[[8],[16],[7],[7],[1],[16],[3],[2],[6],[5],[10],[1],[2],[13],[16],[1],[12],[14],[3],[4],[13],[5],[5],[2],[12],[13],[13],[1],[13],[5],[9],[4],[2],[1],[3],[6],[12],[14],[6],[4],[16],[4],[15],[16],[14],[15],[5],[12],[0],[16],[9],[13],[2],[15],[6],[12],[4],[8],[11],[12],[13],[15],[7],[14],[9],[12],[11],[11],[1],[9],[5],[4],[13],[1],[14],[7],[13],[9],[6],[13],[1],[0],[16],[1],[5],[5],[6],[10],[8],[1],[13],[10],[8],[8],[7],[12],[0],[0],[15],[8],[10],[13],[8],[1],[2],[15],[15],[3],[7],[15],[13],[1],[14],[3],[1],[15],[6],[13],[4],[7],[2],[7],[15],[7],[3],[12],[12],[15],[12],[16],[9],[0],[4],[12],[0],[0],[5],[16],[2],[12],[2],[2],[15],[3],[3],[9],[16],[5],[3],[3],[15],[15],[11],[4],[8],[9],[0],[1],[5],[4],[16],[12],[15],[5],[12],[7],[6],[5],[1],[0],[14],[10],[13],[3],[11],[11],[0],[16],[2],[2],[13],[0],[14],[12],[3],[8],[2],[15],[1],[6],[0],[14],[7],[14],[9],[15],[6],[1],[2],[4],[6],[14],[11],[8],[8],[11],[5],[9],[1],[2],[15],[12],[1],[16],[2],[8],[12],[2],[14],[14],[5],[13],[14],[14],[2],[12],[15],[6],[9],[9],[11],[9],[12],[14],[2],[12],[1],[5],[13],[7],[5],[14],[7],[1],[6],[0],[4],[4],[14],[5],[6],[8],[6],[15],[14],[12],[2],[7],[4],[8],[15],[13],[0],[14],[8],[11],[10],[3],[14],[4],[7],[15],[15],[5],[1],[6],[1],[14],[11],[10],[8],[7],[3],[4],[14],[8],[7],[4],[10],[12],[16],[5],[5],[1],[0],[16],[15],[10],[11],[16],[15],[0],[16],[2],[15],[12],[5],[14],[10],[9],[15],[16],[2],[12],[15],[13],[12],[7],[4],[10],[13],[10],[14],[16],[0],[1],[6],[5],[8],[10],[15],[16],[8],[4],[9],[16],[1],[16],[8],[11],[2],[15],[2],[4],[0],[13],[16],[4],[15],[5],[14],[14],[4],[3],[2],[1],[3],[9],[15],[11],[1],[2],[15],[16],[0],[16],[7],[5],[9],[4],[11],[12],[0],[4],[0],[8],[12],[14],[10],[5],[11],[3],[4],[12],[7],[12],[2],[0],[10],[7],[3],[10],[14],[10],[15],[2],[14],[5],[14],[16],[15],[9],[8],[1],[5],[9],[7],[15],[16],[3],[12],[13],[15],[4],[10],[7],[0],[4],[2],[1],[14],[10],[13],[7],[2],[4],[5],[2],[9],[6],[8],[15],[15],[12],[14],[0],[13],[1],[0],[12],[8],[10],[4],[3],[9],[10],[16],[0],[12],[3],[3],[13],[14],[14],[1],[13],[12],[11],[12],[16],[2],[1],[0],[14],[3],[15],[13],[15],[2],[12],[2],[7],[4],[3],[1],[4],[3],[15],[7],[12],[7],[5],[1],[7],[14],[7],[12],[13],[16],[9],[15],[12],[1],[3],[14],[12],[11],[12],[0],[6],[15],[9],[11],[1],[6],[16],[4],[8],[11],[8],[3],[4]],[[3],[7],[11],[11],[15],[8],[2],[13],[6],[7],[0],[15],[3],[10],[16],[14],[14],[8],[9],[10],[15],[3],[15],[15],[1],[11],[9],[1],[10],[1],[6],[10],[0],[9],[13],[7],[11],[3],[6],[2],[5],[16],[4],[11],[7],[0],[6],[1],[4],[9],[7],[8],[3],[15],[3],[15],[13],[10],[0],[2],[14],[1],[10],[2],[4],[16],[0],[6],[6],[16],[2],[9],[8],[4],[12],[1],[9],[4],[2],[16],[3],[9],[5],[2],[15],[3],[1],[6],[11],[13],[12],[11],[0],[3],[15],[8],[9],[0],[8],[12],[4],[1],[16],[7],[7],[3],[2],[5],[10],[14],[7],[11],[15],[12],[15],[1],[8],[13],[8],[10],[4],[4],[13],[12],[4],[5],[5],[16],[8],[4],[16],[9],[2],[10],[11],[5],[15],[5],[13],[14],[7],[3],[10],[7],[15],[10],[5],[0],[5],[6],[9],[4],[5],[13],[0],[8],[0],[11],[6],[15],[10],[14],[5],[3],[2],[9],[8],[11],[11],[16],[0],[8],[15],[0],[0],[14],[10],[8],[9],[16],[11],[0],[14],[6],[14],[7],[11],[11],[5],[1],[10],[14],[6],[8],[16],[10],[7],[9],[11],[0],[9],[0],[2],[7],[5],[4],[11],[8],[8],[0],[16],[13],[14],[11],[1],[15],[16],[3],[5],[7],[9],[1],[7],[2],[14],[10],[7],[14],[14],[5],[13],[4],[7],[14],[3],[7],[0],[15],[5],[15],[4],[1],[3],[6],[5],[11],[2],[11],[7],[8],[2],[10],[13],[2],[15],[2],[7],[8],[1],[9],[5],[6],[15],[15],[5],[16],[9],[15],[15],[8],[14],[15],[7],[15],[8],[2],[13],[8],[15],[6],[12],[14],[13],[16],[10],[10],[2],[4],[14],[5],[14],[4],[12],[9],[5],[1],[1],[13],[0],[4],[5],[8],[13],[8],[14],[11],[11],[2],[14],[2],[9],[13],[4],[4],[6],[3],[9],[2],[10],[1],[8],[3],[9],[7],[12],[14],[14],[3],[14],[4],[15],[8],[10],[4],[15],[14],[11],[0],[5],[1],[6],[4],[2],[16],[16],[1],[13],[10],[14],[14],[8],[16],[11],[7],[4],[12],[9],[5],[14],[2],[16],[2],[9],[15],[8],[16],[4],[11],[16],[10],[14],[8],[2],[5],[15],[0],[0],[10],[15],[16],[11],[2],[8],[12],[14],[16],[6],[4],[2],[0],[8],[9],[13],[12],[6],[7],[12],[4],[8],[5],[12],[16],[14],[11],[12],[13],[13],[9],[14],[5],[0],[3],[0],[13],[15],[13],[13],[12],[7],[13],[10],[15],[1],[15],[10],[1],[9],[6],[0],[7],[7],[14],[11],[7],[7],[12],[2],[7],[9],[1],[14],[6],[12],[5],[16],[12],[16],[16],[0],[6],[4],[15],[9],[7],[13],[9],[6],[8],[13],[1],[0],[14],[9],[2],[13],[14],[12],[10],[14],[15],[4],[11],[11],[15],[1],[13],[8],[12],[13],[4],[14],[14],[4],[3],[9],[1],[14],[3],[15],[15],[12],[3],[6],[1],[6],[11],[16],[0],[2],[1],[5],[15],[8],[10],[15],[4],[13],[5],[6],[2],[8],[11]],[[9],[6],[14],[7],[10],[4],[12],[4],[7],[8],[3],[15],[2],[13],[10],[5],[1],[16],[10],[8],[13],[14],[2],[8],[10],[8],[16],[9],[16],[16],[1],[15],[5],[2],[5],[14],[0],[7],[4],[10],[5],[10],[16],[4],[15],[1],[5],[13],[12],[5],[0],[9],[6],[5],[14],[8],[10],[4],[3],[12],[13],[9],[15],[6],[11],[10],[1],[13],[0],[3],[4],[2],[1],[0],[4],[12],[1],[0],[10],[8],[13],[5],[15],[16],[6],[12],[7],[11],[8],[5],[4],[0],[6],[4],[15],[14],[11],[13],[12],[6],[6],[3],[16],[5],[2],[11],[11],[9],[3],[7],[14],[7],[11],[13],[7],[16],[15],[8],[5],[13],[16],[8],[11],[16],[6],[12],[4],[9],[5],[13],[16],[14],[15],[1],[8],[0],[14],[11],[16],[0],[6],[5],[16],[9],[1],[6],[5],[15],[2],[0],[4],[10],[6],[8],[5],[15],[1],[13],[1],[10],[5],[3],[9],[3],[8],[2],[11],[13],[0],[10],[5],[16],[5],[8],[0],[2],[16],[8],[14],[1],[1],[10],[11],[0],[0],[6],[15],[11],[2],[5],[14],[11],[12],[0],[0],[7],[15],[10],[13],[5],[16],[9],[15],[6],[16],[15],[15],[11],[2],[12],[0],[16],[0],[4],[4],[13],[5],[14],[16],[13],[14],[7],[2],[13],[3],[0],[2],[2],[10],[1],[14],[15],[15],[6],[6],[13],[1],[0],[3],[14],[14],[10],[12],[6],[6],[7],[16],[3],[16],[10],[9],[11],[16],[4],[13],[16],[4],[4],[16],[13],[14],[10],[3],[12],[6],[12],[1],[3],[13],[5],[11],[16],[14],[16],[9],[9],[8],[2],[7],[5],[13],[8],[2],[16],[16],[0],[1],[0],[11],[12],[12],[15],[8],[12],[15],[6],[2],[16],[2],[4],[4],[16],[13],[5],[15],[5],[9],[3],[0],[1],[1],[3],[15],[15],[13],[13],[16],[14],[3],[8],[9],[14],[9],[2],[5],[8],[2],[8],[14],[6],[11],[13],[14],[13],[11],[14],[7],[8],[3],[12],[5],[6],[3],[8],[4],[8],[0],[7],[4],[11],[15],[3],[6],[6],[10],[14],[2],[9],[7],[9],[7],[0],[0],[6],[6],[0],[1],[13],[11],[14],[8],[9],[12],[14],[6],[7],[8],[7],[2],[16],[13],[9],[11],[2],[7],[10],[15],[10],[6],[10],[14],[7],[16],[16],[6],[13],[15],[12],[10],[13],[15],[4],[4],[13],[7],[15],[3],[7],[12],[1],[12],[5],[10],[14],[8],[10],[14],[13],[5],[8],[5],[0],[9],[12],[8],[4],[6],[12],[11],[10],[11],[6],[8],[3],[3],[2],[0],[1],[9],[7],[16],[5],[6],[6],[8],[9],[5],[5],[16],[8],[2],[13],[16],[11],[10],[12],[4],[10],[4],[13],[2],[13],[9],[9],[7],[11],[2],[10],[4],[6],[15],[7],[10],[16],[0],[3],[5],[1],[2],[2],[16],[4],[11],[12],[16],[1],[7],[16],[14],[5],[12],[5],[5],[1],[8],[15],[15],[10],[2],[14],[14],[14],[15],[16],[13],[8],[1],[6],[6],[12],[6],[15]],[[12],[9],[11],[0],[7],[1],[5],[15],[11],[8],[0],[13],[6],[8],[3],[12],[15],[7],[7],[11],[15],[6],[11],[2],[16],[0],[1],[4],[14],[14],[3],[4],[5],[4],[13],[2],[14],[12],[8],[14],[12],[8],[5],[1],[6],[5],[13],[10],[4],[3],[2],[11],[3],[8],[2],[3],[8],[15],[12],[4],[1],[4],[11],[4],[5],[16],[6],[8],[16],[14],[15],[10],[14],[8],[13],[15],[2],[1],[10],[8],[6],[1],[7],[8],[12],[0],[5],[11],[0],[13],[15],[5],[1],[16],[2],[11],[2],[10],[9],[14],[3],[5],[16],[2],[14],[14],[3],[9],[10],[2],[8],[15],[12],[7],[6],[14],[13],[15],[8],[13],[13],[13],[12],[11],[16],[4],[1],[0],[15],[16],[0],[1],[2],[2],[6],[7],[0],[1],[0],[5],[6],[10],[16],[10],[3],[10],[7],[14],[0],[2],[0],[14],[7],[8],[13],[13],[4],[0],[5],[0],[1],[14],[0],[0],[5],[11],[3],[9],[2],[13],[4],[8],[13],[11],[8],[16],[11],[13],[2],[14],[1],[4],[3],[9],[11],[13],[13],[9],[4],[9],[1],[1],[6],[2],[7],[4],[7],[10],[7],[3],[0],[6],[5],[13],[9],[12],[5],[11],[9],[11],[5],[9],[4],[1],[10],[16],[13],[9],[3],[1],[12],[10],[3],[5],[14],[12],[11],[9],[1],[3],[7],[5],[12],[14],[2],[9],[9],[5],[4],[9],[0],[13],[4],[11],[16],[5],[14],[10],[7],[1],[10],[12],[2],[12],[13],[6],[2],[11],[5],[5],[9],[4],[6],[15],[4],[6],[15],[6],[10],[10],[6],[0],[10],[6],[5],[9],[11],[5],[14],[0],[5],[8],[3],[3],[16],[10],[5],[8],[15],[6],[2],[2],[5],[1],[0],[5],[8],[0],[6],[1],[3],[13],[1],[14],[11],[13],[10],[15],[12],[16],[15],[14],[4],[5],[8],[10],[14],[14],[2],[1],[3],[6],[7],[12],[9],[1],[8],[7],[0],[12],[7],[8],[1],[7],[10],[4],[10],[11],[5],[3],[12],[4],[6],[1],[9],[8],[0],[0],[3],[11],[12],[8],[6],[3],[4],[0],[2],[4],[3],[13],[12],[2],[5],[1],[2],[4],[0],[14],[0],[0],[3],[5],[1],[14],[12],[13],[3],[9],[12],[8],[13],[16],[9],[12],[3],[14],[7],[16],[6],[13],[12],[13],[4],[1],[13],[0],[1],[4],[9],[11],[8],[5],[7],[9],[7],[4],[12],[7],[5],[14],[14],[11],[3],[9],[1],[4],[13],[4],[9],[8],[16],[16],[1],[13],[11],[13],[3],[8],[3],[9],[10],[12],[15],[5],[4],[11],[11],[13],[3],[7],[8],[9],[7],[8],[3],[14],[16],[16],[13],[1],[3],[16],[2],[9],[0],[16],[9],[8],[10],[9],[13],[11],[2],[7],[14],[15],[6],[16],[15],[14],[9],[5],[7],[0],[13],[4],[0],[6],[0],[3],[0],[14],[12],[7],[16],[8],[2],[15],[15],[6],[16],[13],[1],[15],[11],[9],[5],[10],[13],[10],[15],[4],[11],[3],[1],[3],[9],[1],[14],[15],[16],[9]],[[15],[1],[9],[3],[6],[1],[14],[10],[7],[0],[14],[1],[2],[0],[14],[14],[16],[14],[3],[13],[6],[4],[13],[3],[15],[12],[15],[2],[0],[11],[5],[0],[8],[3],[12],[6],[13],[9],[13],[1],[10],[0],[8],[8],[0],[3],[4],[4],[9],[13],[5],[16],[12],[10],[10],[3],[14],[5],[0],[4],[16],[10],[3],[4],[8],[16],[13],[1],[15],[3],[8],[12],[10],[16],[3],[6],[5],[5],[7],[13],[3],[10],[10],[13],[14],[0],[7],[1],[2],[16],[14],[14],[7],[6],[9],[8],[12],[16],[5],[6],[16],[3],[1],[12],[2],[16],[7],[14],[4],[12],[15],[11],[6],[7],[11],[9],[15],[9],[11],[0],[0],[6],[4],[4],[5],[4],[4],[2],[5],[0],[9],[6],[9],[8],[8],[4],[9],[8],[11],[4],[9],[0],[14],[9],[0],[6],[6],[2],[11],[15],[7],[9],[4],[9],[10],[7],[2],[6],[9],[12],[6],[14],[15],[5],[11],[11],[11],[5],[9],[7],[9],[6],[2],[7],[7],[10],[15],[1],[6],[12],[5],[14],[8],[8],[15],[6],[14],[10],[13],[16],[6],[11],[4],[2],[9],[6],[14],[2],[16],[10],[16],[16],[3],[5],[10],[9],[0],[11],[12],[7],[1],[10],[5],[10],[0],[16],[5],[0],[10],[1],[9],[7],[9],[12],[2],[2],[1],[16],[1],[14],[1],[1],[7],[3],[10],[15],[0],[2],[6],[5],[13],[13],[12],[9],[16],[1],[14],[3],[9],[6],[4],[3],[8],[4],[11],[0],[9],[10],[12],[2],[11],[1],[0],[6],[0],[2],[15],[0],[12],[12],[8],[0],[2],[5],[15],[12],[0],[0],[8],[1],[8],[14],[15],[4],[4],[15],[6],[4],[0],[11],[4],[3],[8],[14],[14],[12],[12],[3],[12],[3],[4],[7],[3],[11],[11],[7],[5],[11],[10],[6],[14],[11],[12],[9],[9],[12],[13],[5],[15],[9],[7],[16],[11],[10],[1],[10],[10],[15],[14],[10],[8],[15],[1],[3],[11],[5],[12],[3],[3],[6],[4],[11],[13],[15],[12],[10],[12],[15],[6],[7],[3],[1],[9],[15],[3],[4],[12],[10],[12],[2],[10],[8],[1],[15],[9],[14],[0],[0],[10],[11],[6],[14],[8],[5],[6],[1],[3],[5],[9],[6],[12],[14],[10],[9],[0],[1],[1],[6],[0],[0],[8],[16],[15],[2],[2],[12],[3],[9],[4],[1],[7],[11],[5],[2],[6],[12],[0],[7],[1],[14],[4],[16],[14],[2],[7],[8],[4],[15],[7],[9],[14],[1],[8],[4],[5],[14],[12],[6],[4],[10],[9],[5],[13],[10],[9],[11],[13],[14],[4],[6],[11],[10],[0],[8],[9],[1],[16],[12],[6],[14],[0],[12],[14],[14],[11],[16],[5],[10],[2],[13],[5],[15],[11],[15],[9],[15],[16],[7],[10],[3],[6],[2],[5],[13],[13],[9],[9],[0],[4],[2],[4],[3],[12],[13],[16],[1],[10],[11],[3],[7],[11],[1],[5],[3],[2],[9],[1],[14],[16],[13],[1],[9],[6],[12],[9],[16],[16],[2],[7],[0],[0],[15]],[[10],[13],[3],[4],[12],[12],[0],[1],[0],[4],[8],[2],[11],[12],[9],[16],[5],[2],[1],[6],[11],[6],[16],[13],[13],[11],[12],[14],[8],[3],[10],[13],[14],[16],[11],[2],[13],[14],[15],[12],[8],[5],[2],[4],[8],[11],[12],[16],[6],[13],[7],[5],[13],[13],[8],[9],[11],[10],[7],[2],[3],[7],[15],[12],[4],[5],[12],[14],[3],[11],[13],[12],[8],[16],[1],[6],[2],[12],[13],[0],[5],[8],[8],[1],[3],[12],[11],[13],[10],[13],[16],[5],[3],[1],[10],[14],[0],[2],[4],[12],[0],[16],[2],[7],[9],[9],[1],[5],[12],[13],[2],[16],[14],[13],[8],[10],[2],[9],[14],[3],[12],[8],[5],[12],[6],[11],[14],[7],[0],[6],[7],[1],[10],[8],[14],[2],[8],[12],[8],[13],[7],[13],[2],[7],[13],[0],[7],[7],[10],[6],[14],[16],[1],[10],[11],[2],[12],[11],[15],[2],[1],[4],[12],[14],[12],[9],[16],[16],[14],[6],[2],[1],[7],[2],[3],[0],[6],[15],[1],[7],[15],[1],[10],[7],[8],[10],[13],[13],[3],[12],[14],[11],[11],[10],[7],[7],[2],[15],[6],[4],[9],[16],[12],[6],[8],[13],[1],[1],[12],[3],[8],[14],[2],[12],[16],[11],[4],[0],[10],[1],[14],[7],[4],[12],[16],[5],[15],[8],[0],[1],[11],[1],[0],[1],[16],[13],[4],[5],[16],[12],[10],[6],[3],[8],[10],[3],[12],[14],[16],[5],[6],[9],[5],[13],[6],[16],[10],[1],[4],[10],[0],[2],[4],[12],[10],[3],[10],[7],[2],[16],[6],[2],[13],[1],[13],[7],[15],[7],[13],[11],[12],[9],[7],[6],[14],[14],[1],[5],[4],[8],[7],[13],[7],[1],[11],[4],[8],[9],[15],[8],[4],[3],[4],[15],[9],[16],[10],[15],[6],[1],[14],[4],[3],[9],[0],[9],[13],[8],[5],[3],[0],[14],[12],[2],[2],[9],[3],[0],[6],[8],[6],[4],[5],[14],[8],[1],[15],[5],[6],[14],[8],[0],[6],[11],[9],[14],[16],[4],[7],[3],[7],[5],[14],[14],[12],[12],[13],[0],[7],[2],[1],[7],[8],[4],[1],[14],[11],[7],[3],[4],[1],[0],[9],[5],[12],[9],[15],[6],[12],[4],[9],[10],[3],[11],[6],[4],[1],[12],[13],[16],[0],[3],[2],[9],[5],[5],[10],[2],[1],[1],[11],[8],[5],[0],[13],[3],[16],[7],[4],[12],[7],[11],[9],[16],[1],[14],[7],[1],[2],[0],[11],[1],[11],[6],[1],[6],[4],[2],[9],[16],[5],[7],[11],[16],[5],[9],[1],[10],[13],[16],[16],[16],[2],[15],[0],[15],[2],[12],[11],[0],[16],[8],[0],[8],[12],[7],[5],[3],[6],[10],[4],[0],[7],[2],[7],[12],[2],[14],[5],[13],[4],[7],[2],[16],[7],[10],[10],[14],[12],[14],[4],[1],[0],[9],[9],[15],[8],[10],[15],[6],[6],[15],[4],[12],[7],[13],[2],[11],[14],[0],[12],[12],[16],[1],[6],[0],[15],[0],[4],[9],[2],[0]],[[3],[5],[15],[6],[12],[16],[10],[12],[15],[13],[15],[7],[13],[3],[5],[16],[9],[1],[3],[6],[12],[1],[16],[0],[16],[11],[14],[6],[5],[4],[12],[12],[16],[16],[14],[15],[14],[6],[8],[6],[9],[12],[5],[15],[2],[13],[12],[5],[5],[10],[1],[13],[15],[9],[16],[7],[14],[13],[2],[2],[11],[15],[10],[15],[4],[2],[1],[16],[8],[1],[9],[4],[6],[7],[2],[15],[4],[13],[15],[12],[5],[9],[16],[9],[7],[6],[9],[6],[1],[2],[15],[14],[7],[8],[1],[3],[16],[2],[4],[3],[13],[8],[0],[13],[14],[12],[2],[15],[2],[3],[5],[0],[15],[13],[7],[5],[6],[3],[11],[5],[1],[15],[7],[1],[13],[7],[11],[4],[3],[10],[5],[1],[3],[10],[12],[7],[0],[0],[15],[1],[14],[10],[1],[15],[0],[16],[2],[3],[10],[5],[15],[7],[15],[3],[8],[3],[10],[11],[6],[9],[2],[6],[12],[11],[11],[10],[14],[11],[13],[11],[10],[1],[13],[12],[15],[11],[4],[6],[8],[10],[6],[0],[2],[9],[12],[5],[0],[5],[16],[8],[5],[6],[11],[16],[12],[2],[4],[16],[1],[0],[12],[12],[8],[13],[8],[4],[13],[8],[10],[1],[8],[12],[8],[6],[15],[1],[0],[12],[10],[4],[7],[9],[1],[5],[1],[9],[3],[13],[9],[4],[12],[12],[7],[5],[5],[1],[10],[16],[16],[5],[9],[4],[8],[15],[11],[11],[15],[8],[8],[13],[5],[13],[7],[10],[11],[10],[7],[4],[11],[9],[12],[8],[2],[3],[11],[7],[1],[9],[12],[0],[1],[3],[0],[13],[4],[6],[2],[8],[16],[11],[13],[11],[0],[9],[16],[16],[16],[13],[2],[12],[5],[8],[5],[15],[15],[12],[7],[11],[11],[1],[7],[11],[0],[15],[11],[10],[4],[0],[5],[5],[2],[14],[4],[6],[15],[4],[14],[4],[7],[10],[5],[16],[16],[15],[2],[15],[5],[2],[11],[9],[13],[11],[11],[9],[14],[12],[3],[5],[7],[9],[10],[13],[11],[0],[7],[11],[11],[0],[7],[4],[11],[5],[4],[0],[9],[11],[6],[6],[13],[14],[0],[15],[11],[8],[16],[13],[1],[1],[0],[8],[14],[5],[12],[13],[0],[12],[1],[16],[12],[3],[10],[0],[14],[2],[6],[14],[16],[8],[3],[11],[6],[10],[12],[9],[14],[4],[5],[1],[2],[14],[2],[5],[7],[3],[5],[9],[13],[14],[8],[1],[10],[7],[16],[13],[16],[15],[3],[11],[16],[11],[16],[3],[12],[7],[5],[9],[16],[14],[3],[6],[14],[4],[15],[10],[16],[0],[11],[5],[10],[15],[3],[2],[15],[9],[10],[0],[10],[6],[15],[9],[5],[7],[2],[7],[13],[13],[1],[1],[5],[8],[7],[6],[16],[7],[13],[7],[8],[6],[9],[15],[4],[1],[2],[6],[2],[6],[7],[7],[5],[14],[4],[9],[1],[10],[10],[12],[5],[6],[12],[7],[15],[11],[12],[13],[7],[11],[16],[1],[8],[8],[13],[9],[15],[11],[6],[6],[2],[9],[1],[13],[9],[1]],[[13],[0],[11],[14],[8],[0],[3],[5],[14],[10],[11],[14],[10],[16],[1],[3],[14],[10],[4],[0],[2],[10],[10],[12],[2],[5],[3],[9],[9],[2],[3],[6],[6],[4],[3],[14],[9],[7],[7],[13],[3],[6],[6],[10],[8],[11],[1],[7],[9],[6],[14],[6],[7],[7],[5],[0],[3],[12],[13],[9],[15],[4],[5],[8],[12],[2],[3],[3],[9],[16],[10],[6],[4],[13],[14],[3],[6],[15],[14],[12],[10],[5],[0],[7],[11],[0],[15],[7],[10],[5],[6],[15],[16],[7],[7],[2],[8],[1],[16],[2],[3],[4],[15],[10],[11],[14],[10],[3],[6],[13],[2],[3],[6],[15],[15],[5],[7],[12],[15],[12],[15],[2],[4],[2],[15],[13],[14],[9],[1],[16],[4],[7],[0],[4],[16],[5],[2],[11],[14],[5],[2],[6],[8],[2],[9],[0],[4],[16],[10],[16],[13],[6],[11],[9],[10],[4],[15],[15],[13],[7],[15],[16],[4],[0],[2],[2],[13],[2],[16],[9],[3],[14],[14],[9],[10],[3],[16],[7],[1],[13],[0],[8],[6],[13],[9],[1],[3],[2],[6],[5],[6],[1],[3],[16],[3],[7],[15],[0],[5],[12],[9],[4],[8],[8],[7],[10],[1],[3],[4],[4],[11],[14],[6],[2],[10],[7],[9],[8],[2],[0],[4],[1],[3],[1],[4],[16],[10],[12],[5],[3],[7],[5],[8],[1],[13],[7],[9],[14],[14],[2],[0],[3],[0],[12],[15],[15],[12],[7],[8],[14],[15],[12],[0],[16],[6],[8],[3],[8],[10],[10],[2],[12],[10],[16],[12],[13],[4],[12],[10],[10],[3],[6],[2],[0],[8],[9],[12],[14],[0],[10],[8],[8],[2],[9],[2],[14],[14],[11],[2],[0],[1],[14],[6],[3],[16],[9],[2],[10],[15],[1],[0],[6],[2],[6],[8],[14],[14],[14],[11],[12],[16],[6],[1],[7],[14],[9],[4],[12],[16],[16],[8],[5],[9],[6],[16],[3],[0],[11],[8],[14],[12],[2],[9],[14],[0],[15],[9],[3],[5],[1],[14],[16],[8],[15],[14],[16],[8],[5],[7],[12],[6],[16],[5],[7],[1],[16],[14],[12],[0],[2],[13],[3],[16],[3],[11],[10],[10],[13],[10],[10],[3],[7],[8],[14],[12],[9],[14],[0],[15],[7],[16],[0],[8],[13],[15],[16],[11],[8],[16],[4],[7],[7],[0],[7],[8],[0],[4],[14],[12],[4],[5],[16],[1],[16],[10],[4],[6],[5],[14],[5],[10],[8],[16],[0],[2],[15],[3],[15],[4],[13],[16],[14],[3],[12],[16],[2],[9],[9],[13],[0],[4],[7],[10],[16],[1],[2],[9],[11],[12],[1],[13],[11],[16],[0],[8],[1],[14],[8],[14],[3],[1],[3],[15],[10],[9],[1],[2],[7],[11],[9],[1],[3],[3],[10],[7],[4],[0],[1],[13],[1],[10],[14],[16],[2],[5],[11],[4],[9],[5],[10],[1],[6],[8],[13],[10],[11],[11],[11],[3],[13],[6],[12],[13],[1],[1],[5],[15],[1],[11],[14],[9],[8],[7],[14],[11],[0],[3],[8],[10],[1],[13],[4]],[[16],[1],[10],[7],[2],[3],[9],[5],[15],[8],[7],[10],[8],[12],[15],[6],[3],[10],[9],[13],[12],[2],[8],[15],[5],[12],[16],[9],[8],[0],[11],[15],[5],[5],[10],[3],[16],[2],[0],[5],[13],[1],[10],[8],[8],[3],[11],[13],[2],[1],[9],[15],[8],[12],[9],[7],[7],[16],[14],[11],[9],[8],[13],[1],[13],[7],[13],[13],[12],[15],[15],[8],[13],[12],[0],[7],[0],[11],[3],[10],[13],[11],[16],[15],[9],[1],[14],[13],[9],[4],[14],[1],[0],[10],[12],[14],[2],[6],[8],[8],[8],[6],[9],[7],[5],[8],[11],[8],[8],[14],[9],[13],[4],[14],[12],[10],[13],[2],[0],[1],[13],[7],[0],[11],[9],[2],[10],[2],[9],[8],[15],[5],[14],[13],[1],[0],[7],[13],[8],[8],[12],[14],[2],[13],[0],[13],[7],[8],[4],[1],[15],[11],[7],[0],[14],[13],[10],[1],[8],[8],[11],[8],[14],[15],[3],[11],[9],[11],[7],[5],[9],[12],[11],[2],[15],[1],[2],[0],[14],[0],[8],[4],[9],[2],[8],[11],[14],[4],[14],[16],[10],[0],[0],[5],[8],[12],[11],[3],[9],[16],[7],[1],[8],[3],[16],[0],[5],[13],[14],[3],[3],[0],[8],[1],[16],[0],[1],[6],[2],[6],[9],[10],[2],[3],[16],[14],[16],[12],[4],[4],[3],[14],[12],[0],[3],[3],[14],[2],[15],[13],[6],[8],[4],[1],[15],[10],[14],[14],[6],[15],[6],[9],[2],[5],[14],[15],[4],[6],[13],[8],[7],[14],[1],[12],[3],[7],[1],[12],[1],[3],[1],[15],[6],[11],[13],[14],[11],[5],[11],[5],[8],[14],[8],[5],[2],[5],[14],[12],[8],[16],[2],[6],[15],[2],[7],[8],[3],[7],[12],[1],[0],[2],[4],[0],[15],[8],[4],[9],[14],[15],[12],[5],[0],[4],[3],[14],[3],[12],[7],[6],[2],[9],[11],[0],[9],[16],[7],[14],[0],[2],[14],[10],[10],[1],[8],[12],[7],[4],[7],[15],[14],[6],[3],[12],[11],[11],[9],[11],[1],[13],[11],[6],[7],[2],[9],[11],[14],[6],[5],[8],[2],[7],[7],[9],[10],[5],[0],[14],[1],[7],[2],[16],[6],[11],[5],[12],[3],[3],[10],[13],[4],[13],[15],[4],[13],[16],[6],[14],[7],[13],[0],[2],[10],[12],[2],[2],[11],[6],[1],[16],[1],[9],[5],[11],[11],[16],[12],[5],[13],[11],[7],[10],[8],[4],[14],[1],[4],[7],[6],[12],[1],[12],[11],[14],[15],[4],[4],[5],[12],[15],[14],[13],[3],[11],[0],[9],[3],[2],[2],[3],[16],[7],[14],[1],[5],[16],[11],[0],[0],[0],[13],[5],[1],[8],[4],[13],[3],[3],[12],[10],[10],[9],[8],[7],[5],[7],[4],[10],[16],[12],[3],[14],[14],[8],[5],[5],[10],[6],[1],[11],[2],[11],[9],[8],[2],[4],[8],[11],[5],[0],[9],[9],[1],[9],[0],[14],[8],[11],[7],[7],[10],[0],[8],[4],[14],[5],[16],[10],[10],[5],[2],[15]],[[7],[4],[4],[7],[11],[8],[11],[8],[2],[11],[9],[7],[8],[9],[10],[6],[8],[0],[9],[15],[4],[14],[11],[13],[3],[1],[0],[2],[4],[16],[15],[3],[13],[6],[7],[9],[16],[2],[10],[6],[13],[1],[11],[1],[16],[1],[12],[16],[12],[6],[16],[5],[10],[4],[6],[8],[16],[0],[15],[12],[4],[6],[1],[16],[7],[8],[4],[1],[0],[4],[15],[7],[13],[13],[8],[6],[16],[6],[7],[13],[13],[9],[7],[11],[1],[16],[5],[16],[5],[6],[16],[9],[2],[13],[9],[16],[11],[12],[13],[8],[13],[1],[2],[4],[12],[12],[2],[10],[3],[4],[16],[7],[0],[1],[12],[11],[10],[8],[3],[8],[13],[2],[13],[1],[11],[9],[16],[14],[3],[1],[7],[16],[6],[15],[15],[10],[12],[11],[0],[14],[7],[4],[2],[13],[7],[2],[14],[11],[7],[5],[14],[12],[15],[16],[6],[6],[7],[1],[12],[10],[7],[1],[11],[8],[0],[14],[16],[6],[14],[2],[0],[8],[0],[7],[14],[11],[1],[0],[12],[4],[1],[3],[16],[4],[16],[8],[9],[14],[6],[6],[1],[11],[4],[16],[6],[7],[8],[16],[6],[14],[1],[11],[13],[14],[7],[5],[13],[10],[11],[14],[3],[7],[3],[16],[6],[3],[2],[4],[13],[14],[6],[16],[3],[11],[14],[15],[12],[6],[2],[2],[13],[1],[2],[13],[2],[11],[6],[1],[8],[7],[9],[1],[14],[3],[0],[6],[13],[10],[8],[10],[4],[16],[5],[8],[13],[2],[4],[3],[8],[9],[3],[12],[10],[13],[12],[7],[9],[12],[2],[0],[0],[10],[2],[16],[15],[9],[12],[6],[13],[16],[8],[7],[0],[14],[11],[15],[7],[3],[2],[7],[11],[6],[3],[4],[9],[4],[15],[1],[11],[0],[6],[8],[0],[16],[5],[5],[9],[5],[12],[13],[13],[9],[8],[0],[7],[13],[5],[10],[11],[4],[5],[5],[11],[13],[6],[8],[14],[4],[10],[6],[10],[9],[7],[16],[0],[16],[15],[0],[5],[16],[14],[16],[16],[1],[4],[3],[5],[16],[0],[8],[14],[1],[7],[4],[11],[15],[14],[2],[15],[6],[4],[3],[10],[9],[15],[1],[10],[14],[6],[4],[9],[14],[5],[3],[5],[4],[2],[5],[5],[1],[6],[16],[1],[8],[15],[3],[6],[11],[8],[13],[15],[12],[3],[15],[8],[5],[10],[15],[8],[5],[5],[5],[9],[16],[9],[8],[3],[16],[10],[12],[10],[5],[13],[15],[12],[11],[9],[0],[13],[8],[7],[11],[12],[2],[8],[11],[13],[7],[3],[4],[12],[1],[9],[4],[16],[16],[13],[5],[4],[5],[10],[15],[2],[9],[3],[13],[12],[8],[9],[8],[3],[6],[8],[6],[2],[16],[5],[14],[3],[1],[1],[10],[15],[15],[16],[2],[15],[12],[12],[1],[5],[0],[6],[7],[0],[11],[11],[5],[0],[3],[2],[2],[16],[0],[6],[1],[9],[4],[7],[7],[11],[0],[0],[3],[10],[3],[6],[14],[1],[5],[6],[8],[6],[5],[0],[8],[13],[16],[7],[5],[12],[15]],[[16],[4],[8],[5],[7],[4],[6],[5],[11],[1],[15],[5],[0],[0],[3],[8],[3],[10],[1],[3],[12],[1],[1],[0],[4],[15],[8],[3],[7],[6],[2],[13],[1],[4],[14],[9],[3],[16],[4],[0],[7],[3],[8],[10],[12],[1],[4],[5],[11],[10],[15],[13],[13],[12],[6],[4],[11],[3],[14],[9],[3],[11],[0],[4],[0],[11],[6],[1],[6],[4],[4],[10],[15],[14],[15],[3],[3],[7],[6],[4],[16],[9],[7],[15],[0],[13],[9],[3],[13],[15],[8],[13],[10],[3],[2],[8],[1],[2],[0],[11],[9],[8],[1],[11],[15],[3],[0],[0],[16],[5],[7],[1],[13],[0],[10],[2],[10],[16],[2],[3],[13],[10],[6],[5],[4],[3],[9],[2],[14],[2],[14],[9],[2],[1],[1],[6],[15],[6],[10],[6],[11],[8],[2],[2],[3],[7],[14],[16],[6],[1],[7],[4],[4],[9],[10],[16],[0],[4],[1],[8],[6],[12],[14],[10],[15],[0],[3],[16],[3],[4],[4],[12],[4],[12],[0],[12],[12],[1],[12],[12],[15],[0],[6],[6],[13],[2],[5],[5],[0],[11],[14],[15],[6],[14],[0],[14],[15],[4],[4],[16],[4],[8],[15],[14],[10],[9],[7],[7],[11],[8],[5],[1],[16],[4],[3],[12],[10],[8],[15],[3],[0],[16],[13],[6],[3],[8],[5],[4],[1],[0],[11],[16],[9],[14],[13],[13],[16],[6],[5],[10],[9],[5],[0],[1],[7],[7],[11],[11],[0],[7],[15],[1],[8],[7],[1],[12],[9],[8],[14],[8],[0],[16],[7],[13],[12],[16],[14],[5],[13],[8],[0],[10],[5],[0],[1],[11],[14],[14],[5],[11],[8],[14],[11],[16],[16],[2],[10],[0],[4],[13],[11],[2],[5],[14],[15],[3],[1],[4],[0],[1],[15],[10],[10],[6],[5],[9],[10],[7],[7],[8],[4],[11],[16],[2],[8],[12],[13],[15],[3],[10],[7],[11],[10],[3],[1],[3],[15],[16],[0],[16],[6],[14],[1],[11],[0],[12],[11],[7],[5],[2],[2],[3],[4],[13],[1],[5],[0],[16],[4],[12],[10],[3],[11],[15],[16],[11],[3],[6],[2],[15],[0],[7],[15],[7],[16],[13],[1],[4],[5],[8],[0],[9],[12],[1],[12],[4],[15],[3],[12],[2],[4],[11],[12],[6],[13],[13],[13],[14],[5],[13],[9],[12],[2],[2],[14],[8],[6],[6],[7],[10],[15],[1],[15],[7],[6],[6],[2],[14],[2],[6],[12],[0],[4],[3],[8],[10],[10],[10],[1],[8],[12],[3],[12],[2],[9],[9],[14],[7],[16],[4],[13],[2],[1],[13],[5],[16],[1],[8],[7],[6],[15],[16],[7],[1],[3],[2],[12],[5],[5],[4],[8],[11],[12],[3],[14],[7],[15],[8],[16],[4],[4],[9],[11],[1],[1],[8],[11],[3],[7],[3],[12],[7],[7],[8],[2],[11],[5],[12],[14],[5],[16],[14],[4],[14],[4],[2],[3],[13],[14],[10],[8],[15],[9],[2],[4],[4],[6],[16],[14],[16],[16],[3],[8],[13],[14],[4],[8],[10],[7],[1],[6],[14]],[[13],[11],[15],[5],[2],[2],[11],[5],[12],[11],[3],[12],[15],[15],[3],[10],[16],[12],[15],[8],[16],[8],[14],[16],[3],[7],[9],[10],[6],[3],[7],[9],[5],[0],[14],[1],[13],[12],[4],[12],[12],[4],[1],[0],[12],[10],[15],[11],[3],[11],[4],[0],[10],[6],[14],[10],[4],[7],[13],[13],[3],[6],[6],[14],[8],[8],[5],[1],[15],[1],[4],[6],[12],[3],[13],[6],[5],[16],[2],[10],[11],[1],[4],[14],[15],[11],[4],[7],[2],[2],[3],[8],[0],[2],[7],[11],[7],[10],[11],[10],[0],[5],[1],[16],[8],[2],[12],[10],[12],[4],[12],[10],[6],[11],[12],[9],[0],[1],[13],[11],[1],[6],[16],[7],[5],[5],[10],[13],[13],[5],[1],[15],[16],[7],[12],[15],[1],[7],[3],[16],[15],[5],[11],[0],[13],[4],[3],[4],[4],[15],[15],[4],[1],[14],[13],[10],[4],[5],[8],[4],[15],[5],[10],[11],[7],[9],[6],[3],[5],[4],[14],[2],[13],[0],[12],[16],[1],[2],[7],[8],[11],[10],[2],[10],[2],[12],[1],[12],[13],[7],[9],[8],[5],[6],[4],[9],[2],[11],[7],[1],[11],[7],[1],[2],[5],[11],[12],[7],[15],[4],[16],[15],[13],[1],[0],[7],[6],[11],[14],[11],[6],[9],[2],[8],[0],[12],[1],[16],[2],[5],[4],[8],[7],[15],[1],[1],[5],[6],[14],[6],[3],[13],[0],[10],[1],[15],[9],[3],[13],[8],[11],[16],[4],[8],[14],[3],[10],[11],[16],[0],[14],[12],[4],[8],[13],[5],[16],[3],[12],[4],[4],[0],[7],[14],[7],[3],[6],[1],[4],[0],[3],[16],[7],[12],[13],[13],[12],[3],[1],[10],[10],[14],[5],[7],[7],[6],[12],[7],[16],[9],[3],[2],[10],[0],[15],[3],[6],[7],[0],[11],[7],[14],[12],[10],[3],[0],[15],[5],[2],[2],[8],[0],[8],[1],[3],[11],[15],[0],[11],[7],[10],[14],[6],[15],[6],[3],[6],[12],[13],[8],[16],[4],[6],[4],[14],[10],[0],[14],[0],[3],[6],[8],[11],[16],[4],[0],[2],[3],[3],[2],[13],[15],[8],[1],[8],[13],[13],[11],[1],[7],[6],[3],[2],[5],[13],[7],[8],[4],[15],[2],[8],[15],[3],[14],[11],[1],[4],[13],[5],[7],[2],[16],[0],[1],[7],[14],[16],[15],[0],[1],[5],[12],[9],[2],[15],[13],[16],[1],[2],[12],[14],[10],[16],[2],[7],[16],[8],[16],[4],[16],[15],[3],[8],[2],[15],[4],[16],[11],[8],[8],[11],[4],[11],[6],[5],[7],[13],[13],[8],[9],[2],[6],[15],[12],[16],[9],[7],[3],[16],[1],[15],[2],[16],[10],[0],[8],[16],[14],[10],[15],[0],[14],[9],[10],[14],[9],[5],[3],[6],[7],[10],[15],[4],[13],[5],[0],[1],[16],[14],[9],[2],[10],[5],[14],[5],[12],[4],[15],[8],[9],[2],[13],[5],[13],[5],[12],[2],[8],[11],[6],[10],[12],[0],[2],[4],[6],[0],[6],[0],[0],[11],[2]],[[15],[14],[10],[14],[12],[16],[13],[11],[16],[4],[9],[6],[16],[4],[4],[7],[13],[6],[16],[1],[1],[14],[10],[14],[14],[2],[0],[13],[3],[0],[14],[8],[13],[7],[8],[8],[8],[16],[1],[11],[9],[15],[0],[8],[12],[5],[16],[11],[7],[4],[5],[10],[5],[7],[6],[15],[4],[14],[10],[15],[8],[8],[8],[11],[8],[8],[13],[14],[0],[12],[7],[3],[10],[5],[4],[8],[13],[7],[10],[7],[0],[16],[11],[11],[4],[10],[12],[4],[11],[12],[8],[0],[11],[1],[8],[3],[0],[7],[0],[13],[4],[9],[12],[15],[13],[5],[12],[5],[1],[7],[15],[12],[13],[9],[12],[11],[7],[15],[10],[11],[1],[9],[7],[13],[6],[0],[15],[16],[3],[13],[1],[10],[11],[5],[4],[6],[7],[9],[2],[4],[4],[8],[1],[0],[14],[10],[1],[11],[9],[9],[3],[11],[3],[7],[0],[6],[14],[1],[3],[7],[2],[12],[14],[9],[11],[8],[0],[11],[2],[10],[6],[5],[16],[12],[8],[14],[5],[4],[16],[10],[3],[12],[13],[5],[1],[1],[14],[4],[0],[0],[11],[8],[2],[7],[8],[12],[11],[8],[1],[11],[6],[14],[15],[1],[4],[0],[1],[0],[5],[10],[0],[13],[4],[16],[15],[15],[11],[2],[2],[7],[7],[4],[14],[8],[3],[2],[16],[11],[4],[7],[6],[13],[11],[14],[12],[3],[7],[1],[12],[3],[9],[1],[10],[3],[11],[16],[0],[13],[5],[10],[16],[16],[11],[4],[0],[7],[3],[15],[7],[15],[4],[4],[0],[8],[9],[12],[15],[16],[15],[13],[15],[8],[5],[10],[9],[11],[0],[15],[2],[14],[2],[0],[6],[6],[9],[8],[9],[0],[4],[11],[1],[9],[7],[9],[7],[3],[3],[0],[0],[15],[15],[3],[0],[6],[6],[8],[6],[15],[11],[5],[1],[7],[16],[5],[14],[7],[11],[11],[0],[15],[14],[16],[10],[6],[9],[7],[3],[12],[15],[3],[8],[2],[0],[0],[6],[3],[12],[2],[16],[2],[13],[0],[15],[8],[4],[16],[5],[10],[4],[9],[1],[14],[2],[2],[14],[14],[7],[10],[11],[12],[14],[15],[7],[7],[6],[11],[8],[4],[2],[14],[6],[12],[15],[14],[13],[13],[8],[15],[5],[7],[0],[14],[5],[16],[14],[8],[2],[4],[2],[5],[0],[8],[16],[8],[4],[12],[11],[10],[2],[13],[11],[14],[7],[0],[5],[6],[3],[7],[0],[11],[10],[1],[6],[13],[13],[3],[7],[8],[1],[7],[1],[11],[6],[1],[10],[4],[9],[13],[0],[4],[1],[10],[3],[6],[1],[1],[11],[0],[12],[0],[8],[15],[12],[15],[6],[8],[6],[4],[10],[5],[13],[10],[9],[8],[8],[4],[6],[4],[10],[8],[12],[0],[13],[3],[16],[9],[13],[11],[12],[0],[15],[12],[5],[14],[6],[5],[11],[13],[3],[15],[12],[16],[11],[6],[11],[5],[6],[1],[5],[2],[4],[9],[16],[2],[1],[12],[4],[2],[12],[14],[7],[5],[11],[5],[7],[4],[0],[10],[12],[3],[15],[15]],[[1],[15],[7],[0],[12],[5],[3],[11],[0],[3],[3],[14],[15],[15],[16],[6],[8],[12],[6],[3],[11],[12],[12],[3],[3],[8],[9],[11],[9],[10],[0],[11],[1],[5],[15],[9],[4],[14],[9],[7],[1],[12],[4],[13],[3],[0],[13],[16],[15],[0],[7],[12],[6],[13],[12],[9],[2],[5],[12],[12],[1],[11],[8],[15],[12],[13],[12],[10],[16],[10],[14],[9],[11],[4],[14],[4],[4],[8],[1],[13],[9],[7],[6],[7],[3],[2],[11],[16],[2],[2],[3],[7],[3],[0],[9],[4],[9],[16],[15],[8],[3],[5],[7],[9],[8],[3],[0],[6],[2],[9],[0],[5],[14],[6],[7],[10],[15],[1],[16],[15],[10],[9],[5],[7],[8],[5],[13],[6],[6],[16],[14],[2],[16],[4],[2],[16],[7],[9],[6],[1],[2],[3],[11],[15],[7],[1],[10],[9],[5],[6],[0],[16],[14],[10],[12],[8],[1],[7],[9],[2],[4],[2],[0],[6],[1],[2],[8],[1],[1],[11],[11],[2],[11],[14],[5],[14],[9],[16],[12],[7],[7],[9],[9],[6],[1],[13],[15],[7],[0],[14],[0],[11],[3],[8],[6],[13],[15],[13],[6],[4],[12],[5],[3],[0],[4],[15],[9],[8],[0],[9],[10],[8],[16],[9],[3],[0],[12],[4],[2],[8],[1],[0],[14],[3],[1],[5],[13],[7],[9],[12],[11],[13],[10],[5],[4],[9],[14],[5],[5],[15],[16],[4],[9],[1],[11],[8],[10],[3],[11],[10],[14],[11],[5],[3],[1],[1],[1],[2],[3],[10],[13],[13],[4],[0],[16],[2],[2],[4],[12],[5],[10],[6],[10],[6],[7],[15],[7],[10],[10],[16],[12],[8],[1],[8],[16],[9],[15],[4],[6],[16],[0],[3],[9],[11],[10],[16],[13],[0],[7],[5],[3],[14],[6],[14],[10],[8],[14],[16],[10],[15],[1],[8],[15],[6],[4],[16],[1],[3],[12],[14],[9],[5],[5],[15],[14],[16],[10],[6],[13],[16],[4],[12],[1],[8],[10],[6],[3],[16],[12],[15],[11],[12],[11],[6],[13],[15],[15],[2],[1],[0],[3],[16],[9],[2],[4],[9],[1],[0],[13],[0],[9],[14],[0],[12],[15],[3],[3],[4],[16],[3],[16],[1],[3],[8],[16],[15],[9],[12],[2],[5],[2],[3],[12],[2],[14],[6],[0],[12],[0],[0],[1],[7],[13],[7],[16],[1],[8],[14],[13],[5],[16],[1],[0],[10],[3],[11],[5],[1],[3],[6],[6],[6],[6],[13],[8],[1],[8],[5],[4],[2],[7],[15],[7],[2],[14],[10],[11],[14],[3],[15],[10],[4],[13],[8],[15],[7],[11],[14],[14],[14],[4],[9],[2],[2],[16],[2],[16],[9],[6],[14],[16],[13],[12],[4],[3],[5],[9],[6],[13],[7],[1],[13],[4],[3],[3],[15],[1],[10],[13],[0],[4],[16],[15],[7],[9],[3],[11],[7],[13],[10],[12],[6],[8],[4],[7],[12],[8],[15],[2],[1],[12],[12],[4],[6],[8],[5],[12],[10],[14],[11],[6],[5],[15],[5],[10],[2],[5],[8],[9],[2],[10],[3]]]
ZW = 545
def setup_inputs(rng):
    return {"z": rng.standard_normal((N, 128, ZW), dtype=np.float32)}
def reference(z):
    y = np.zeros((N, 128, T), np.float64)
    fill = [0] * N
    for r in range(N):
        for t in range(T):
            for e in ROUTE[r][t]:
                y[r][:, t] += z[e][:, fill[e]].astype(np.float64)
                fill[e] += 1
    return {"y": y.astype(z.dtype)}

@@ -1,0 +1,287 @@
+import numpy as np
+from concourse.bass import DstId, RemoteDMATransfer
+import comms_topo
+
+USE_FAR = True
+USE_OWN = True
+LAG = 60
+OWNER, HOLDER = 4, 6
+RELAYS = (6, 2, 7, 3)
+NEAR = (0, 1, 2, 3, 5, 6, 7)
+
+SCRATCH = {
+    "zs": ("sbuf", [128, 545], "float32"),
+    "st": ("sbuf", [128, 512], "float32"),
+}
+SEMAPHORES = ["ld", "win", "pc", "arr", "snt", "sto"]
+CACHE = {}
+
+
+def masks_for(n, eng):
+    per = 1
+    while per * 2 * n <= eng:
+        per *= 2
+    return [((1 << per) - 1) << (i * per) for i in range(n)], per
+
+
+def split_classes(x, sm, ncc, nnc):
+    best = None
+    for a in range(ncc + 1):
+        h = nnc + ncc - a
+        if (x and not a) or (sm and not h):
+            continue
+        v = max(-(-x // a) if x else 0, -(-sm // h) if sm else 0)
+        if best is None or v < best[0]:
+            best = (v, a)
+    return best
+
+
+def choose_far(n, tt, cnt, par, ncc, nnc):
+    opts = []
+    for e in range(n):
+        o = [((), 0)]
+        for s in range(n):
+            for m in range(1, n - s + 1):
+                rng = tuple(range(s, s + m))
+                if e in rng:
+                    break
+                x = sum(cnt[e][r] for r in rng if par[r] != par[e])
+                sp = split_classes(x, sum(cnt[e][r] for r in rng) - x, ncc[e], nnc[e])
+                if sp is not None:
+                    o.append((rng, sp[0]))
+        opts.append(o)
+    sel = [o[0] for o in opts]
+    left = [tt] * n
+    for sweep in range(12):
+        before = list(sel)
+        for e in range(n):
+            for r in sel[e][0]:
+                left[r] += cnt[e][r]
+            best = None
+            for o in opts[e]:
+                sel[e] = o
+                for r in o[0]:
+                    left[r] -= cnt[e][r]
+                v = sum((8 * q / 7.0 + LAG) ** 8 for q in left) + sum((16.0 * q[1]) ** 8 for q in sel)
+                for r in o[0]:
+                    left[r] += cnt[e][r]
+                if best is None or v < best[0]:
+                    best = (v, o)
+            sel[e] = best[1]
+            for r in sel[e][0]:
+                left[r] -= cnt[e][r]
+        if sel == before:
+            break
+    return [v[0] for v in sel]
+
+
+def scatter_calls(cols, eng):
+    calls = []
+    for i in range(0, len(cols), eng):
+        part = cols[i:i + eng]
+        ms, per = masks_for(len(part), eng)
+        calls.append([(b, c, 1, d, "st", t, ms[j], "arr") for j, (c, b, t, d) in enumerate(part)])
+    return calls
+
+
+def build(tables, cores):
+    if "p" in CACHE:
+        return CACHE["p"]
+    n, tt, zw, route = len(cores), tables["T"], tables["ZW"], tables["ROUTE"]
+    tok = [[[] for r in range(n)] for e in range(n)]
+    for r in range(n):
+        for t in range(tt):
+            tok[route[r][t][0]][r].append(t)
+    cnt = [[len(tok[e][r]) for r in range(n)] for e in range(n)]
+    off = [[sum(cnt[e][:r]) for r in range(n)] for e in range(n)]
+    par = [comms_topo.chip(c) % 2 for c in cores]
+    base = [c - c % 8 for c in cores]
+    steps = {}
+
+    def add(core, step):
+        steps.setdefault(core, []).append(step)
+
+    far_cc = [[] for e in range(n)]
+    far_nc = [[] for e in range(n)]
+    if USE_FAR:
+        for p in (0, 1):
+            snd = [e for e in range(n) if par[e] == p]
+            idle = [b + i for b in range(0, 256, 8) if b not in base and comms_topo.chip(b) % 2 == p for i in range(8)]
+            cc = [c for c in idle if comms_topo.may_write(c, c ^ 8)]
+            nc = [c for c in idle if not comms_topo.may_write(c, c ^ 8)]
+            for i, e in enumerate(snd):
+                far_cc[e] = cc[i::len(snd)]
+                far_nc[e] = nc[i::len(snd)]
+    own = 1 if USE_OWN else 0
+    sel = choose_far(n, tt, cnt, par, [len(v) for v in far_cc], [len(v) + own for v in far_nc])
+
+    arr = [0] * n
+    far_jobs = [[] for e in range(n)]
+    bypass = set()
+    for e in range(n):
+        xs = [(r, i) for r in sel[e] if par[r] != par[e] for i in range(cnt[e][r])]
+        ss = [(r, i) for r in sel[e] if par[r] == par[e] for i in range(cnt[e][r])]
+        for r in sel[e]:
+            bypass.add((e, r))
+        if not sel[e]:
+            continue
+        a = split_classes(len(xs), len(ss), len(far_cc[e]), len(far_nc[e]) + own)[1]
+        for seq, hl in ((ss, ([cores[e]] if own else []) + far_nc[e] + far_cc[e][a:]), (xs, far_cc[e][:a])):
+            pos = 0
+            for j, c in enumerate(hl):
+                m = len(seq) // len(hl) + (1 if j < len(seq) % len(hl) else 0)
+                if m:
+                    far_jobs[e].append((c, seq[pos:pos + m]))
+                pos += m
+
+    pieces = [[] for e in range(n)]
+    got = {}
+    for r in range(n):
+        seq = [(e, i) for e in range(n) if e != r and (e, r) not in bypass for i in range(cnt[e][r])]
+        tot = len(seq) + cnt[r][r]
+        hs = min(len(seq), max(0, int(round(tot / 7.0)) - cnt[r][r]))
+        rest = len(seq) - hs
+        pos = 0
+        k = 0
+        for h in NEAR:
+            if h == HOLDER:
+                m = hs
+            else:
+                m = rest // 6 + (1 if k < rest % 6 else 0)
+                k += 1
+            seg = seq[pos:pos + m]
+            pos += m
+            i = 0
+            while i < len(seg):
+                j = i
+                while j < len(seg) and seg[j][0] == seg[i][0]:
+                    j += 1
+                e, i0, i1 = seg[i][0], seg[i][1], seg[j - 1][1] + 1
+                pc = {"e": e, "r": r, "k0": off[e][r] + i0, "k1": off[e][r] + i1, "dst": base[r] + h,
+                      "toks": tok[e][r][i0:i1]}
+                pieces[e].append(pc)
+                got.setdefault(base[r] + h, []).append(pc)
+                i = j
+
+    relay_calls = {}
+    relay_win = {}
+    for e in range(n):
+        oc = cores[e]
+        add(oc, ("load",))
+        items = sorted(pieces[e] + [{"self": 1, "k0": off[e][e], "k1": off[e][e] + cnt[e][e]}], key=lambda d: d["k0"])
+        m = len(items)
+        best = None
+        for a in range(m + 1):
+            for b in range(a, m + 1):
+                for c in range(b, m + 1):
+                    gs = [items[0:a], items[a:b], items[b:c], items[c:m]]
+                    mp = max(sum(1 for d in gr if "self" not in d) for gr in gs)
+                    wd = max((gr[-1]["k1"] - gr[0]["k0"]) if gr else 0 for gr in gs)
+                    sc = (0 if mp <= 4 else 1 if mp <= 8 else 2, wd, mp)
+                    if best is None or sc < best[0]:
+                        best = (sc, gs)
+        gs = [gr for gr in best[1] if gr]
+        wb = best[0][1]
+        free = [c for c in RELAYS if c != HOLDER]
+        trs = []
+        ms, per = masks_for(len(gs), 16)
+        for gi, gr in enumerate(gs):
+            rc = base[e] + (HOLDER if any("self" in d for d in gr) else free.pop(0))
+            ws = min(gr[0]["k0"], zw - wb)
+            trs.append(("zs", ws, wb, rc, "zs", 0, ms[gi], "win"))
+            relay_win[rc] = (ws, per)
+            ps = [d for d in gr if "self" not in d]
+            calls = []
+            for i in range(0, len(ps), 8):
+                part = ps[i:i + 8]
+                w = max(d["k1"] - d["k0"] for d in part)
+                pm, pper = masks_for(len(part), 8)
+                for j, d in enumerate(part):
+                    s = min(d["k0"], ws + wb - w)
+                    d["w"], d["delta"], d["src"], d["mask"], d["inc"] = w, d["k0"] - s, s - ws, pm[j], pper
+                calls.append(part)
+            relay_calls[rc] = calls
+        add(oc, ("call", trs))
+        fj = [(c, q) for (c, q) in far_jobs[e] if c != oc]
+        if fj:
+            span = [(off[e][q[0][0]] + q[0][1], off[e][q[-1][0]] + q[-1][1] + 1) for (c, q) in fj]
+            w = max(k1 - k0 for (k0, k1) in span)
+            fm, fper = masks_for(len(fj), 8)
+            trs = []
+            for j, (c, q) in enumerate(fj):
+                s = min(span[j][0], zw - w)
+                trs.append(("zs", s, w, c, "st", 0, fm[j], "pc"))
+                add(c, ("wait", "pc", fper))
+                cols = [(off[e][r] + i - s, "st", tok[e][r][i], cores[r]) for (r, i) in q]
+                for call in scatter_calls(cols, 8):
+                    add(c, ("call", call))
+            add(oc, ("call", trs))
+        for (c, q) in far_jobs[e]:
+            if c == oc:
+                cols = [(off[e][r] + i, "zs", tok[e][r][i], cores[r]) for (r, i) in q]
+                for call in scatter_calls(cols, 8):
+                    add(oc, ("call", call))
+
+    for r in range(n):
+        for h in NEAR:
+            c = base[r] + h
+            if c in relay_win:
+                ws, per = relay_win[c]
+                add(c, ("wait", "win", per))
+                for part in relay_calls[c]:
+                    add(c, ("call", [("zs", d["src"], d["w"], d["dst"], "st", None, d["mask"], "pc", d) for d in part]))
+                if h == HOLDER:
+                    cols = [(off[r][r] - ws + i, "zs", t, cores[r]) for i, t in enumerate(tok[r][r])]
+                    for call in scatter_calls(cols, 16):
+                        add(c, ("call", call))
+    for c, ps in got.items():
+        pos, inc, cols = 0, 0, []
+        for d in ps:
+            d["slot"] = pos
+            cols += [(pos + d["delta"] + i, "st", t, c - c % 8 + OWNER) for i, t in enumerate(d["toks"])]
+            pos += d["w"]
+            inc += d["inc"]
+        add(c, ("wait", "pc", inc))
+        for call in scatter_calls(cols, 16):
+            add(c, ("call", call))
+    rank_of = dict((c, i) for i, c in enumerate(cores))
+    for c, st in steps.items():
+        for si, s in enumerate(st):
+            if s[0] != "call":
+                continue
+            s = ("call", [(t[0], t[1], t[2], t[3], t[4], t[8]["slot"], t[6], t[7]) if len(t) == 9 else t for t in s[1]])
+            st[si] = s
+            for t in s[1]:
+                if t[7] == "arr":
+                    arr[rank_of[t[3]]] += bin(t[6]).count("1")
+    for e in range(n):
+        add(cores[e], ("store", arr[e]))
+    CACHE["p"] = steps
+    return steps
+
+
+def rank_program(g, core, T, topo):
+    steps = build(T.tables, list(T.cores)).get(core)
+    if not steps:
+        return
+    sent = 0
+    for s in steps:
+        if s[0] == "load":
+            g.sync.dma_start(T.zs[:], T.z[:]).then_inc(T.sem.ld, 16)
+            g.wait_ge(T.sem.ld, 16)
+        elif s[0] == "wait":
+            g.wait_ge(T.sem[s[1]], s[2])
+        elif s[0] == "call":
+            trs = []
+            for (sb, s0, w, dc, db, d0, m, rs) in s[1]:
+                rid, pid = topo.addr(dc, core)
+                trs.append(RemoteDMATransfer(dst_ids=[DstId(rid=rid, pnc=pid)], dma_engine_mask=m,
+                                             remote_sem=T.sem[rs], src=T[sb][:, s0:s0 + w], dst=T[db][:, d0:d0 + w]))
+                sent += bin(m).count("1")
+            g.remote_dma_fused(trs, local_sem=T.sem.snt)
+        elif s[0] == "store":
+            g.sync.wait_ge(T.sem.arr, s[1])
+            g.sync.dma_start(T.y[:], T.st[:]).then_inc(T.sem.sto, 16)
+            g.sync.wait_ge(T.sem.sto, 16)
+    if sent:
+        g.wait_ge(T.sem.snt, sent)

@@ -4,7 +4,8 @@ import comms_topo
 
 USE_FAR = True
 USE_OWN = True
-LAG = 60
+LAG = 0
+NS, CHUNK = 4, 128
 OWNER, HOLDER = 4, 6
 RELAYS = (6, 2, 7, 3)
 NEAR = (0, 1, 2, 3, 5, 6, 7)
@@ -13,7 +14,7 @@ SCRATCH = {
     "zs": ("sbuf", [128, 545], "float32"),
     "st": ("sbuf", [128, 512], "float32"),
 }
-SEMAPHORES = ["ld", "win", "pc", "arr", "snt", "sto"]
+SEMAPHORES = ["ld", "win", "pc", "snt"] + ["a%d" % i for i in range(NS)] + ["s%d" % i for i in range(NS)]
 CACHE = {}
 
 
@@ -76,11 +77,12 @@ def choose_far(n, tt, cnt, par, ncc, nnc):
 
 
 def scatter_calls(cols, eng):
+    cols = sorted(cols, key=lambda v: v[2] // CHUNK)
     calls = []
     for i in range(0, len(cols), eng):
         part = cols[i:i + eng]
         ms, per = masks_for(len(part), eng)
-        calls.append([(b, c, 1, d, "st", t, ms[j], "arr") for j, (c, b, t, d) in enumerate(part)])
+        calls.append([(b, c, 1, d, "st", t, ms[j], "a%d" % (t // CHUNK)) for j, (c, b, t, d) in enumerate(part)])
     return calls
 
 
@@ -115,7 +117,7 @@ def build(tables, cores):
     own = 1 if USE_OWN else 0
     sel = choose_far(n, tt, cnt, par, [len(v) for v in far_cc], [len(v) + own for v in far_nc])
 
-    arr = [0] * n
+    arr = [[0] * NS for e in range(n)]
     far_jobs = [[] for e in range(n)]
     bypass = set()
     for e in range(n):
@@ -252,8 +254,8 @@ def build(tables, cores):
             s = ("call", [(t[0], t[1], t[2], t[3], t[4], t[8]["slot"], t[6], t[7]) if len(t) == 9 else t for t in s[1]])
             st[si] = s
             for t in s[1]:
-                if t[7] == "arr":
-                    arr[rank_of[t[3]]] += bin(t[6]).count("1")
+                if t[7][0] == "a":
+                    arr[rank_of[t[3]]][int(t[7][1:])] += bin(t[6]).count("1")
     for e in range(n):
         add(cores[e], ("store", arr[e]))
     CACHE["p"] = steps
@@ -280,8 +282,13 @@ def rank_program(g, core, T, topo):
                 sent += bin(m).count("1")
             g.remote_dma_fused(trs, local_sem=T.sem.snt)
         elif s[0] == "store":
-            g.sync.wait_ge(T.sem.arr, s[1])
-            g.sync.dma_start(T.y[:], T.st[:]).then_inc(T.sem.sto, 16)
-            g.sync.wait_ge(T.sem.sto, 16)
+            for i in range(NS):
+                q = g.sync if i % 2 == 0 else g.scalar
+                q.wait_ge(T.sem["a%d" % i], s[1][i])
+                q.dma_start(T.y[:, i * CHUNK:(i + 1) * CHUNK],
+                            T.st[:, i * CHUNK:(i + 1) * CHUNK]).then_inc(T.sem["s%d" % i], 16)
+            for i in range(NS):
+                q = g.sync if i % 2 == 0 else g.scalar
+                q.wait_ge(T.sem["s%d" % i], 16)
     if sent:
         g.wait_ge(T.sem.snt, sent)

import numpy as np
from concourse.bass import DstId, RemoteDMATransfer
import comms_topo

USE_FAR = True
USE_OWN = True
LAG = 0
NS, CHUNK = 4, 128
OWNER, HOLDER = 4, 6
RELAYS = (6, 2, 7, 3)
NEAR = (0, 1, 2, 3, 5, 6, 7)

SCRATCH = {
    "zs": ("sbuf", [128, 545], "float32"),
    "st": ("sbuf", [128, 512], "float32"),
}
SEMAPHORES = ["ld", "win", "pc", "snt"] + ["a%d" % i for i in range(NS)] + ["s%d" % i for i in range(NS)]
CACHE = {}


def masks_for(n, eng):
    per = 1
    while per * 2 * n <= eng:
        per *= 2
    return [((1 << per) - 1) << (i * per) for i in range(n)], per


def split_classes(x, sm, ncc, nnc):
    best = None
    for a in range(ncc + 1):
        h = nnc + ncc - a
        if (x and not a) or (sm and not h):
            continue
        v = max(-(-x // a) if x else 0, -(-sm // h) if sm else 0)
        if best is None or v < best[0]:
            best = (v, a)
    return best


def choose_far(n, tt, cnt, par, ncc, nnc):
    opts = []
    for e in range(n):
        o = [((), 0)]
        for s in range(n):
            for m in range(1, n - s + 1):
                rng = tuple(range(s, s + m))
                if e in rng:
                    break
                x = sum(cnt[e][r] for r in rng if par[r] != par[e])
                sp = split_classes(x, sum(cnt[e][r] for r in rng) - x, ncc[e], nnc[e])
                if sp is not None:
                    o.append((rng, sp[0]))
        opts.append(o)
    sel = [o[0] for o in opts]
    left = [tt] * n
    for sweep in range(12):
        before = list(sel)
        for e in range(n):
            for r in sel[e][0]:
                left[r] += cnt[e][r]
            best = None
            for o in opts[e]:
                sel[e] = o
                for r in o[0]:
                    left[r] -= cnt[e][r]
                v = sum((8 * q / 7.0 + LAG) ** 8 for q in left) + sum((16.0 * q[1]) ** 8 for q in sel)
                for r in o[0]:
                    left[r] += cnt[e][r]
                if best is None or v < best[0]:
                    best = (v, o)
            sel[e] = best[1]
            for r in sel[e][0]:
                left[r] -= cnt[e][r]
        if sel == before:
            break
    return [v[0] for v in sel]


def scatter_calls(cols, eng):
    cols = sorted(cols, key=lambda v: v[2] // CHUNK)
    calls = []
    for i in range(0, len(cols), eng):
        part = cols[i:i + eng]
        ms, per = masks_for(len(part), eng)
        calls.append([(b, c, 1, d, "st", t, ms[j], "a%d" % (t // CHUNK)) for j, (c, b, t, d) in enumerate(part)])
    return calls


def build(tables, cores):
    if "p" in CACHE:
        return CACHE["p"]
    n, tt, zw, route = len(cores), tables["T"], tables["ZW"], tables["ROUTE"]
    tok = [[[] for r in range(n)] for e in range(n)]
    for r in range(n):
        for t in range(tt):
            tok[route[r][t][0]][r].append(t)
    cnt = [[len(tok[e][r]) for r in range(n)] for e in range(n)]
    off = [[sum(cnt[e][:r]) for r in range(n)] for e in range(n)]
    par = [comms_topo.chip(c) % 2 for c in cores]
    base = [c - c % 8 for c in cores]
    steps = {}

    def add(core, step):
        steps.setdefault(core, []).append(step)

    far_cc = [[] for e in range(n)]
    far_nc = [[] for e in range(n)]
    if USE_FAR:
        for p in (0, 1):
            snd = [e for e in range(n) if par[e] == p]
            idle = [b + i for b in range(0, 256, 8) if b not in base and comms_topo.chip(b) % 2 == p for i in range(8)]
            cc = [c for c in idle if comms_topo.may_write(c, c ^ 8)]
            nc = [c for c in idle if not comms_topo.may_write(c, c ^ 8)]
            for i, e in enumerate(snd):
                far_cc[e] = cc[i::len(snd)]
                far_nc[e] = nc[i::len(snd)]
    own = 1 if USE_OWN else 0
    sel = choose_far(n, tt, cnt, par, [len(v) for v in far_cc], [len(v) + own for v in far_nc])

    arr = [[0] * NS for e in range(n)]
    far_jobs = [[] for e in range(n)]
    bypass = set()
    for e in range(n):
        xs = [(r, i) for r in sel[e] if par[r] != par[e] for i in range(cnt[e][r])]
        ss = [(r, i) for r in sel[e] if par[r] == par[e] for i in range(cnt[e][r])]
        for r in sel[e]:
            bypass.add((e, r))
        if not sel[e]:
            continue
        a = split_classes(len(xs), len(ss), len(far_cc[e]), len(far_nc[e]) + own)[1]
        for seq, hl in ((ss, ([cores[e]] if own else []) + far_nc[e] + far_cc[e][a:]), (xs, far_cc[e][:a])):
            pos = 0
            for j, c in enumerate(hl):
                m = len(seq) // len(hl) + (1 if j < len(seq) % len(hl) else 0)
                if m:
                    far_jobs[e].append((c, seq[pos:pos + m]))
                pos += m

    pieces = [[] for e in range(n)]
    got = {}
    for r in range(n):
        seq = [(e, i) for e in range(n) if e != r and (e, r) not in bypass for i in range(cnt[e][r])]
        tot = len(seq) + cnt[r][r]
        hs = min(len(seq), max(0, int(round(tot / 7.0)) - cnt[r][r]))
        rest = len(seq) - hs
        pos = 0
        k = 0
        for h in NEAR:
            if h == HOLDER:
                m = hs
            else:
                m = rest // 6 + (1 if k < rest % 6 else 0)
                k += 1
            seg = seq[pos:pos + m]
            pos += m
            i = 0
            while i < len(seg):
                j = i
                while j < len(seg) and seg[j][0] == seg[i][0]:
                    j += 1
                e, i0, i1 = seg[i][0], seg[i][1], seg[j - 1][1] + 1
                pc = {"e": e, "r": r, "k0": off[e][r] + i0, "k1": off[e][r] + i1, "dst": base[r] + h,
                      "toks": tok[e][r][i0:i1]}
                pieces[e].append(pc)
                got.setdefault(base[r] + h, []).append(pc)
                i = j

    relay_calls = {}
    relay_win = {}
    for e in range(n):
        oc = cores[e]
        add(oc, ("load",))
        items = sorted(pieces[e] + [{"self": 1, "k0": off[e][e], "k1": off[e][e] + cnt[e][e]}], key=lambda d: d["k0"])
        m = len(items)
        best = None
        for a in range(m + 1):
            for b in range(a, m + 1):
                for c in range(b, m + 1):
                    gs = [items[0:a], items[a:b], items[b:c], items[c:m]]
                    mp = max(sum(1 for d in gr if "self" not in d) for gr in gs)
                    wd = max((gr[-1]["k1"] - gr[0]["k0"]) if gr else 0 for gr in gs)
                    sc = (0 if mp <= 4 else 1 if mp <= 8 else 2, wd, mp)
                    if best is None or sc < best[0]:
                        best = (sc, gs)
        gs = [gr for gr in best[1] if gr]
        wb = best[0][1]
        free = [c for c in RELAYS if c != HOLDER]
        trs = []
        ms, per = masks_for(len(gs), 16)
        for gi, gr in enumerate(gs):
            rc = base[e] + (HOLDER if any("self" in d for d in gr) else free.pop(0))
            ws = min(gr[0]["k0"], zw - wb)
            trs.append(("zs", ws, wb, rc, "zs", 0, ms[gi], "win"))
            relay_win[rc] = (ws, per)
            ps = [d for d in gr if "self" not in d]
            calls = []
            for i in range(0, len(ps), 8):
                part = ps[i:i + 8]
                w = max(d["k1"] - d["k0"] for d in part)
                pm, pper = masks_for(len(part), 8)
                for j, d in enumerate(part):
                    s = min(d["k0"], ws + wb - w)
                    d["w"], d["delta"], d["src"], d["mask"], d["inc"] = w, d["k0"] - s, s - ws, pm[j], pper
                calls.append(part)
            relay_calls[rc] = calls
        add(oc, ("call", trs))
        fj = [(c, q) for (c, q) in far_jobs[e] if c != oc]
        if fj:
            span = [(off[e][q[0][0]] + q[0][1], off[e][q[-1][0]] + q[-1][1] + 1) for (c, q) in fj]
            w = max(k1 - k0 for (k0, k1) in span)
            fm, fper = masks_for(len(fj), 8)
            trs = []
            for j, (c, q) in enumerate(fj):
                s = min(span[j][0], zw - w)
                trs.append(("zs", s, w, c, "st", 0, fm[j], "pc"))
                add(c, ("wait", "pc", fper))
                cols = [(off[e][r] + i - s, "st", tok[e][r][i], cores[r]) for (r, i) in q]
                for call in scatter_calls(cols, 8):
                    add(c, ("call", call))
            add(oc, ("call", trs))
        for (c, q) in far_jobs[e]:
            if c == oc:
                cols = [(off[e][r] + i, "zs", tok[e][r][i], cores[r]) for (r, i) in q]
                for call in scatter_calls(cols, 8):
                    add(oc, ("call", call))

    for r in range(n):
        for h in NEAR:
            c = base[r] + h
            if c in relay_win:
                ws, per = relay_win[c]
                add(c, ("wait", "win", per))
                for part in relay_calls[c]:
                    add(c, ("call", [("zs", d["src"], d["w"], d["dst"], "st", None, d["mask"], "pc", d) for d in part]))
                if h == HOLDER:
                    cols = [(off[r][r] - ws + i, "zs", t, cores[r]) for i, t in enumerate(tok[r][r])]
                    for call in scatter_calls(cols, 16):
                        add(c, ("call", call))
    for c, ps in got.items():
        pos, inc, cols = 0, 0, []
        for d in ps:
            d["slot"] = pos
            cols += [(pos + d["delta"] + i, "st", t, c - c % 8 + OWNER) for i, t in enumerate(d["toks"])]
            pos += d["w"]
            inc += d["inc"]
        add(c, ("wait", "pc", inc))
        for call in scatter_calls(cols, 16):
            add(c, ("call", call))
    rank_of = dict((c, i) for i, c in enumerate(cores))
    for c, st in steps.items():
        for si, s in enumerate(st):
            if s[0] != "call":
                continue
            s = ("call", [(t[0], t[1], t[2], t[3], t[4], t[8]["slot"], t[6], t[7]) if len(t) == 9 else t for t in s[1]])
            st[si] = s
            for t in s[1]:
                if t[7][0] == "a":
                    arr[rank_of[t[3]]][int(t[7][1:])] += bin(t[6]).count("1")
    for e in range(n):
        add(cores[e], ("store", arr[e]))
    CACHE["p"] = steps
    return steps


def rank_program(g, core, T, topo):
    steps = build(T.tables, list(T.cores)).get(core)
    if not steps:
        return
    sent = 0
    for s in steps:
        if s[0] == "load":
            g.sync.dma_start(T.zs[:], T.z[:]).then_inc(T.sem.ld, 16)
            g.wait_ge(T.sem.ld, 16)
        elif s[0] == "wait":
            g.wait_ge(T.sem[s[1]], s[2])
        elif s[0] == "call":
            trs = []
            for (sb, s0, w, dc, db, d0, m, rs) in s[1]:
                rid, pid = topo.addr(dc, core)
                trs.append(RemoteDMATransfer(dst_ids=[DstId(rid=rid, pnc=pid)], dma_engine_mask=m,
                                             remote_sem=T.sem[rs], src=T[sb][:, s0:s0 + w], dst=T[db][:, d0:d0 + w]))
                sent += bin(m).count("1")
            g.remote_dma_fused(trs, local_sem=T.sem.snt)
        elif s[0] == "store":
            for i in range(NS):
                q = g.sync if i % 2 == 0 else g.scalar
                q.wait_ge(T.sem["a%d" % i], s[1][i])
                q.dma_start(T.y[:, i * CHUNK:(i + 1) * CHUNK],
                            T.st[:, i * CHUNK:(i + 1) * CHUNK]).then_inc(T.sem["s%d" % i], 16)
            for i in range(NS):
                q = g.sync if i % 2 == 0 else g.scalar
                q.wait_ge(T.sem["s%d" % i], 16)
    if sent:
        g.wait_ge(T.sem.snt, sent)
